import numpy as np
import ml_dtypes


def mxq(x, axis, fmt="e4m3"):
    dtype, down = {"e4m3": (ml_dtypes.float8_e4m3fn, 7), "e5m2": (ml_dtypes.float8_e5m2, 14)}[fmt]
    v = np.moveaxis(np.asarray(x, np.float32).astype(ml_dtypes.bfloat16).astype(np.float64), axis, -1)
    blocks = v.reshape(v.shape[:-1] + (-1, 32))
    amax = np.abs(blocks).max(-1, keepdims=True)
    byte = np.maximum(np.where(amax > 0, np.frexp(amax)[1] - 1 + 127, 0) - down, 1)
    scale = np.exp2(byte - 127.0)
    codes = (blocks / scale).astype(np.float32).astype(dtype).astype(np.float64)
    return np.moveaxis((codes * scale).reshape(v.shape), -1, axis)


WIDE = False


def mx_kscale(k):
    if not WIDE:
        return np.ones(k)
    levels = np.array([30, -30])
    if k % 512:
        return np.exp2(np.random.permutation(np.resize(levels, k // 32))).repeat(32)
    a = np.empty((k // 512, 16))
    for p in range(k // 512):
        a[p, :8] = np.random.permutation(np.resize(levels, 8))
        for g in range(8):
            far = levels[np.abs(levels - a[p, g]) >= 10]
            a[p, g + 8] = far[np.random.randint(len(far))]
    return np.exp2(a.ravel()).repeat(32)


def f64(x):
    return np.asarray(x).astype(np.float64)


def striped(idx):
    return np.tile(np.asarray(idx).reshape(-1, 16).T, (8, 1)).astype(np.uint16)


def unstriped(offs):
    return offs[:16].T.reshape(-1).astype(np.int64)


E2M1 = np.array([0.0, 0.5, 1.0, 1.5, 2.0, 3.0, 4.0, 6.0, -0.0, -0.5, -1.0, -1.5, -2.0, -3.0, -4.0, -6.0])


def pack_weight(w, fmt):
    k, n = w.shape
    w = f64(np.asarray(w, np.float32).astype(ml_dtypes.bfloat16)).reshape(k // 32, 32, n)
    amax = np.abs(w).max(1)
    if fmt == "e4m3":
        byte = np.frexp(amax)[1] - 1 + 127 - 7
    else:
        mant, ex = np.frexp(amax / 6.0)
        byte = np.where(mant > 0.5, ex, ex - 1) + 127
    byte = np.clip(np.where(amax > 0, byte, 1), 1, 254)
    scaled = (w * np.exp2(127.0 - byte)[:, None, :]).reshape(k, n).astype(np.float32)
    by_word = np.ascontiguousarray(scaled.reshape(k // 512, 128, 4, n).transpose(0, 1, 3, 2))
    if fmt == "e4m3":
        words = by_word.astype(ml_dtypes.float8_e4m3fn).view(np.uint8)
    else:
        c = by_word.astype(ml_dtypes.float4_e2m1fn).view(np.uint8) & 0xF
        words = (c[..., 0::2] | (c[..., 1::2] << 4)).reshape(k // 512, 128, 2 * n)
    return np.ascontiguousarray(words), np.ascontiguousarray(byte.astype(np.uint8).reshape(k // 512, 16, n))


def unpack_weight(words, scales, fmt):
    g, _, n = scales.shape
    words = np.ascontiguousarray(words).reshape(g, 128, n, -1)
    if fmt == "e4m3":
        vals = words.view(ml_dtypes.float8_e4m3fn).astype(np.float64)
    else:
        nib = np.empty((g, 128, n, 4), np.uint8)
        nib[..., 0::2] = words & 0xF
        nib[..., 1::2] = words >> 4
        vals = E2M1[nib]
    vals = vals * np.repeat(np.exp2(scales.astype(np.float64) - 127.0), 8, axis=1)[..., None]
    return vals.transpose(0, 1, 3, 2).reshape(g * 512, n)


K, T, J, R, C, D, O, N, S = 512, 2048, 256, 512, 512, 512, 256, 256, 1024


def setup_inputs():
    n = np.random.standard_normal
    idx = np.random.permutation(T)[:J]
    idx2 = np.random.permutation(T)[:J]
    idx3 = np.random.permutation(C)[:J]
    idx4 = np.random.permutation(D)[:J]
    idx5 = np.random.permutation(D)[:C]
    idx6 = np.random.permutation(C)[:O]
    idx7 = np.random.permutation(S)[:N]
    fk = mx_kscale(K)
    fr = mx_kscale(R)
    xtp = pack_weight(n((K, T)) / fk[:, None], "e2m1")
    wp = pack_weight(n((K, R)) * 1 / np.sqrt(K) * fk[:, None] * fr, "e4m3")
    vsp = pack_weight(n((R, S)) * 1 / np.sqrt(R) / fr[:, None], "e2m1")
    return {
        "xt_words": xtp[0],
        "xt_scales": xtp[1],
        "w_words": wp[0],
        "w_scales": wp[1],
        "vs_words": vsp[0],
        "vs_scales": vsp[1],
        "offs": striped(idx),
        "offs2": striped(idx2),
        "offs3": striped(idx3),
        "offs4": striped(idx4),
        "offs5": striped(idx5),
        "offs6": striped(idx6),
        "offs7": striped(idx7),
    }


def reference(xt_words, xt_scales, w_words, w_scales, vs_words, vs_scales, offs, offs2, offs3, offs4, offs5, offs6, offs7):
    idx = unstriped(offs)
    idx2 = unstriped(offs2)
    idx3 = unstriped(offs3)
    idx4 = unstriped(offs4)
    idx5 = unstriped(offs5)
    idx6 = unstriped(offs6)
    idx7 = unstriped(offs7)
    xtu = unpack_weight(xt_words, xt_scales, "e2m1")
    wu = unpack_weight(w_words, w_scales, "e4m3")
    vsu = unpack_weight(vs_words, vs_scales, "e2m1")
    xtidxg = xtu[:, idx]
    a = wu.T @ xtidxg
    xtidx2g = xtu[:, idx2]
    b = wu.T @ xtidx2g
    pw = np.zeros((R, C))
    pw[:, idx3] = a
    pv = np.zeros((R, D))
    pv[:, idx4] = b
    pg = np.maximum(pw, pv[:, idx5])
    hid = pg[:, idx6]
    vsidx7g = vsu[:, idx7]
    hidq = mxq(hid, 0, "e5m2")
    y = vsidx7g.T @ hidq
    return y

@@ -1,0 +1,172 @@
+from contextlib import ExitStack
+
+import concourse.mybir as mybir
+
+F32 = mybir.dt.float32
+BF16 = mybir.dt.bfloat16
+I32 = mybir.dt.int32
+U32 = mybir.dt.uint32
+U16 = mybir.dt.uint16
+U8 = mybir.dt.uint8
+E4M3 = mybir.dt.float8_e4m3fn_x4
+E5M2 = mybir.dt.float8_e5m2_x4
+E2M1 = mybir.dt.float4_e2m1fn_x4
+COPY = mybir.ActivationFunctionType.Copy
+MAX = mybir.AluOpType.max
+
+P = 128
+PACK = 4
+K, T, J, R, C, D, O, N, S = 512, 2048, 256, 512, 512, 512, 256, 256, 1024
+
+FLOPS = 2 * K * R * 2 * J + 2 * R * N * O
+
+
+def tile_list_boardsmeet_tied_store_plain_kernel(
+    tc, xt_words, xt_scales, w_words, w_scales, vs_words, vs_scales, offs, offs2, offs3, offs4, offs5, offs6, offs7, out
+):
+    nc = tc.nc
+    with ExitStack() as ctx:
+        lists = ctx.enter_context(tc.tile_pool(name="lists", bufs=1))
+        sb = ctx.enter_context(tc.tile_pool(name="sb", bufs=1))
+        ps = ctx.enter_context(tc.psum_pool(name="ps", bufs=1))
+
+        def load_list(src, name):
+            tile = lists.tile([P, src.shape[1]], U16, name=name)
+            nc.sync.dma_start(tile[:], src)
+            return tile
+
+        def load_scales(queue, tile, src):
+            for q in range(4):
+                queue.dma_start(tile[32 * q : 32 * q + 4, :].bitcast(I32), src[0, 4 * q : 4 * q + 4, :].bitcast(I32))
+
+        xt_w = sb.tile([P, T], U16, name="xt_w", align_bytes=64)
+        xt_s = sb.tile([P, T], U8, name="xt_s", align_bytes=64)
+        w_w = sb.tile([P, R], U32, name="w_w", align_bytes=64)
+        w_s = sb.tile([P, R], U8, name="w_s", align_bytes=64)
+        vs_w = sb.tile([P, S], U16, name="vs_w", align_bytes=64)
+        vs_s = sb.tile([P, S], U8, name="vs_s", align_bytes=64)
+
+        nc.vector.memset(xt_s[:].bitcast(I32), 0)
+        nc.vector.memset(w_s[:].bitcast(I32), 0)
+        nc.sync.dma_start(xt_w[:].bitcast(I32), xt_words[0].bitcast(I32))
+        nc.scalar.dma_start(w_w[:].bitcast(I32), w_words[0].rearrange("p n t -> p (n t)").bitcast(I32))
+        idx_b = load_list(offs2, "idx_b")
+        load_scales(nc.sync, xt_s, xt_scales)
+        load_scales(nc.scalar, w_s, w_scales)
+        idx_a = load_list(offs, "idx_a")
+        put_b = load_list(offs4, "put_b")
+        put_a = load_list(offs3, "put_a")
+        meet = load_list(offs5, "meet")
+        read = load_list(offs6, "read")
+        entry = load_list(offs7, "entry")
+        pv = [sb.tile([P, D], F32, name=f"pv{t}") for t in range(PACK)]
+        pw = [sb.tile([P, C], F32, name=f"pw{t}") for t in range(PACK)]
+        for t in range(PACK):
+            nc.vector.memset(pv[t][:], 0.0)
+        nc.vector.memset(vs_s[:].bitcast(I32), 0)
+        nc.sync.dma_start(vs_w[:].bitcast(I32), vs_words[0].bitcast(I32))
+        load_scales(nc.sync, vs_s, vs_scales)
+        for t in range(PACK):
+            nc.vector.memset(pw[t][:], 0.0)
+
+        wp_w = sb.tile([P, PACK, P], U32, name="wp_w", align_bytes=64)
+        wp_s = sb.tile([P, PACK, P], U8, name="wp_s", align_bytes=64)
+        nc.scalar.copy(wp_w[:].rearrange("p t m -> p m t"), w_w[:].rearrange("p (m t) -> p m t", t=PACK))
+        nc.vector.tensor_copy(wp_s[:].rearrange("p t m -> p m t"), w_s[:].rearrange("p (m t) -> p m t", t=PACK))
+
+        def pick(words, scales, idx, name):
+            gw = sb.tile([P, J], U16, name=name + "_w", align_bytes=64)
+            gs = sb.tile([P, J], U8, name=name + "_s", align_bytes=64)
+            nc.vector.tensor_copy(gw[:], words[:].indirect(idx[:]))
+            nc.vector.tensor_copy(gs[:], scales[:].indirect(idx[:]))
+            return gw, gs
+
+        def first_stage(gw, gs, name):
+            banks = [ps.tile([P, 2, J], F32, name=f"{name}{h}") for h in range(2)]
+            for t in range(PACK):
+                nc.tensor.matmul_mx(
+                    banks[t // 2][:, t % 2, :],
+                    lhsT=wp_w[:, t, :].bitcast(E4M3),
+                    lhsT_scale=wp_s[:, t, :],
+                    rhs=gw[:].bitcast(E2M1),
+                    rhs_scale=gs[:],
+                    start=True,
+                    stop=True,
+                )
+            return banks
+
+        b_banks = first_stage(*pick(xt_w, xt_s, idx_b, "xb"), "b_bank")
+        a_banks = first_stage(*pick(xt_w, xt_s, idx_a, "xa"), "a_bank")
+        vg_w, vg_s = pick(vs_w, vs_s, entry, "vg")
+
+        a_sb = [sb.tile([P, 2, J], F32, name=f"a_sb{h}") for h in range(2)]
+        b_sb = [sb.tile([P, 2, J], F32, name=f"b_sb{h}") for h in range(2)]
+        met = [sb.tile([P, C], F32, name=f"met{t}") for t in range(PACK)]
+        pg = [sb.tile([P, C], F32, name=f"pg{t}") for t in range(PACK)]
+        hid = sb.tile([P, PACK, O], F32, name="hid")
+
+        def on_scalar(dst, src):
+            nc.scalar.activation(dst, src, COPY)
+
+        on_vector = nc.vector.tensor_copy
+
+        def put(move, board, values, idx, t):
+            move(board[t][:].indirect(idx[:]), values[t // 2][:, t % 2, :])
+
+        def look_up(move, t):
+            half = C // 2
+            for h in range(2):
+                move(met[t][:, h * half : (h + 1) * half], pv[t][:].indirect(meet[:, h * half // 16 : (h + 1) * half // 16]))
+
+        def keep_larger(t):
+            nc.vector.tensor_tensor(pg[t][:], pw[t][:], met[t][:], MAX)
+
+        def read_out(move, t):
+            move(hid[:, t, :], pg[t][:].indirect(read[:]))
+
+        nc.scalar.copy(b_sb[0][:], b_banks[0][:])
+        put(on_scalar, pv, b_sb, put_b, 0)
+        nc.vector.tensor_copy(a_sb[0][:], a_banks[0][:])
+        put(on_scalar, pv, b_sb, put_b, 1)
+        put(on_vector, pw, a_sb, put_a, 0)
+        look_up(on_scalar, 0)
+        put(on_vector, pw, a_sb, put_a, 1)
+        nc.scalar.copy(b_sb[1][:], b_banks[1][:])
+        keep_larger(0)
+        look_up(on_scalar, 1)
+        nc.vector.tensor_copy(a_sb[1][:], a_banks[1][:])
+        put(on_scalar, pv, b_sb, put_b, 2)
+        put(on_vector, pw, a_sb, put_a, 2)
+        keep_larger(1)
+        read_out(on_scalar, 0)
+        put(on_scalar, pv, b_sb, put_b, 3)
+        put(on_vector, pw, a_sb, put_a, 3)
+        look_up(on_scalar, 2)
+        look_up(on_vector, 3)
+        read_out(on_scalar, 1)
+        keep_larger(2)
+        keep_larger(3)
+        read_out(on_scalar, 2)
+        read_out(on_vector, 3)
+
+        grouped = sb.tile([P, O, PACK], BF16, name="grouped", align_bytes=64)
+        nc.vector.tensor_copy(grouped[:], hid[:].rearrange("p t o -> p o t"))
+        h_w = sb.tile([P, O], U32, name="h_w", align_bytes=64)
+        h_s = sb.tile([P, O], U8, name="h_s", align_bytes=64)
+        nc.vector.quantize_mx(h_w[:].bitcast(E5M2), h_s[:], grouped[:].rearrange("p o t -> p (o t)"))
+
+        for h, (copy_out, queue) in enumerate(((nc.vector.tensor_copy, nc.sync), (nc.scalar.copy, nc.scalar))):
+            cols = slice(h * P, (h + 1) * P)
+            bank = ps.tile([P, O], F32, name=f"y_bank{h}")
+            nc.tensor.matmul_mx(
+                bank[:],
+                lhsT=vg_w[:, cols].bitcast(E2M1),
+                lhsT_scale=vg_s[:, cols],
+                rhs=h_w[:].bitcast(E5M2),
+                rhs_scale=h_s[:],
+                start=True,
+                stop=True,
+            )
+            y = sb.tile([P, O], F32, name=f"y{h}")
+            copy_out(y[:], bank[:])
+            queue.dma_start(out[cols, :], y[:])

@@ -35,9 +35,9 @@ def tile_list_boardsmeet_tied_store_plain_kernel(
             nc.sync.dma_start(tile[:], src)
             return tile
 
-        def load_scales(queue, tile, src):
-            for q in range(4):
-                queue.dma_start(tile[32 * q : 32 * q + 4, :].bitcast(I32), src[0, 4 * q : 4 * q + 4, :].bitcast(I32))
+        def load_scales(tile, src, quadrants):
+            for q in quadrants:
+                nc.sync.dma_start(tile[32 * q : 32 * q + 4, :].bitcast(I32), src[0, 4 * q : 4 * q + 4, :].bitcast(I32))
 
         xt_w = sb.tile([P, T], U16, name="xt_w", align_bytes=64)
         xt_s = sb.tile([P, T], U8, name="xt_s", align_bytes=64)
@@ -47,27 +47,28 @@ def tile_list_boardsmeet_tied_store_plain_kernel(
         vs_s = sb.tile([P, S], U8, name="vs_s", align_bytes=64)
 
         nc.vector.memset(xt_s[:].bitcast(I32), 0)
-        nc.vector.memset(w_s[:].bitcast(I32), 0)
-        nc.sync.dma_start(xt_w[:].bitcast(I32), xt_words[0].bitcast(I32))
-        nc.scalar.dma_start(w_w[:].bitcast(I32), w_words[0].rearrange("p n t -> p (n t)").bitcast(I32))
+        nc.gpsimd.memset(w_s[:].bitcast(I32), 0)
         idx_b = load_list(offs2, "idx_b")
-        load_scales(nc.sync, xt_s, xt_scales)
-        load_scales(nc.scalar, w_s, w_scales)
+        load_scales(w_s, w_scales, (0, 1))
+        nc.sync.dma_start(xt_w[:].bitcast(I32), xt_words[0].bitcast(I32))
+        load_scales(xt_s, xt_scales, range(4))
+        nc.sync.dma_start(w_w[:].bitcast(I32), w_words[0].rearrange("p n t -> p (n t)").bitcast(I32))
+        load_scales(w_s, w_scales, (2, 3))
         idx_a = load_list(offs, "idx_a")
         put_b = load_list(offs4, "put_b")
+        entry = load_list(offs7, "entry")
+        nc.vector.memset(vs_s[:].bitcast(I32), 0)
+        nc.sync.dma_start(vs_w[:].bitcast(I32), vs_words[0].bitcast(I32))
+        load_scales(vs_s, vs_scales, range(4))
         put_a = load_list(offs3, "put_a")
         meet = load_list(offs5, "meet")
         read = load_list(offs6, "read")
-        entry = load_list(offs7, "entry")
+
         pv = [sb.tile([P, D], F32, name=f"pv{t}") for t in range(PACK)]
         pw = [sb.tile([P, C], F32, name=f"pw{t}") for t in range(PACK)]
         for t in range(PACK):
             nc.vector.memset(pv[t][:], 0.0)
-        nc.vector.memset(vs_s[:].bitcast(I32), 0)
-        nc.sync.dma_start(vs_w[:].bitcast(I32), vs_words[0].bitcast(I32))
-        load_scales(nc.sync, vs_s, vs_scales)
-        for t in range(PACK):
-            nc.vector.memset(pw[t][:], 0.0)
+            nc.gpsimd.memset(pw[t][:], 0.0)
 
         wp_w = sb.tile([P, PACK, P], U32, name="wp_w", align_bytes=64)
         wp_s = sb.tile([P, PACK, P], U8, name="wp_s", align_bytes=64)
@@ -81,11 +82,18 @@ def tile_list_boardsmeet_tied_store_plain_kernel(
             nc.vector.tensor_copy(gs[:], scales[:].indirect(idx[:]))
             return gw, gs
 
-        def first_stage(gw, gs, name):
-            banks = [ps.tile([P, 2, J], F32, name=f"{name}{h}") for h in range(2)]
+        def first_stage(gw, gs, name, groups):
+            sums, copies, parts = [], [], []
+            for g, size in enumerate(groups):
+                bank = ps.tile([P, size, J], F32, name=f"{name}_bank{g}")
+                held = sb.tile([P, size, J], F32, name=f"{name}_sb{g}")
+                copies.append((held, bank))
+                for i in range(size):
+                    sums.append(bank[:, i, :])
+                    parts.append(held[:, i, :])
             for t in range(PACK):
                 nc.tensor.matmul_mx(
-                    banks[t // 2][:, t % 2, :],
+                    sums[t],
                     lhsT=wp_w[:, t, :].bitcast(E4M3),
                     lhsT_scale=wp_s[:, t, :],
                     rhs=gw[:].bitcast(E2M1),
@@ -93,14 +101,13 @@ def tile_list_boardsmeet_tied_store_plain_kernel(
                     start=True,
                     stop=True,
                 )
-            return banks
+            return copies, parts
 
-        b_banks = first_stage(*pick(xt_w, xt_s, idx_b, "xb"), "b_bank")
-        a_banks = first_stage(*pick(xt_w, xt_s, idx_a, "xa"), "a_bank")
-        vg_w, vg_s = pick(vs_w, vs_s, entry, "vg")
+        b_copies, b = first_stage(*pick(xt_w, xt_s, idx_b, "xb"), "b", (1, 1, 2))
+        a_copies, a = first_stage(*pick(xt_w, xt_s, idx_a, "xa"), "a", (2, 2))
+        vg_w = sb.tile([P, N], U16, name="vg_w", align_bytes=64)
+        vg_s = sb.tile([P, N], U8, name="vg_s", align_bytes=64)
 
-        a_sb = [sb.tile([P, 2, J], F32, name=f"a_sb{h}") for h in range(2)]
-        b_sb = [sb.tile([P, 2, J], F32, name=f"b_sb{h}") for h in range(2)]
         met = [sb.tile([P, C], F32, name=f"met{t}") for t in range(PACK)]
         pg = [sb.tile([P, C], F32, name=f"pg{t}") for t in range(PACK)]
         hid = sb.tile([P, PACK, O], F32, name="hid")
@@ -110,63 +117,66 @@ def tile_list_boardsmeet_tied_store_plain_kernel(
 
         on_vector = nc.vector.tensor_copy
 
+        def empty(move, pair):
+            move(pair[0][:], pair[1][:])
+
         def put(move, board, values, idx, t):
-            move(board[t][:].indirect(idx[:]), values[t // 2][:, t % 2, :])
+            move(board[t][:].indirect(idx[:]), values[t])
+
+        def listed(idx, cols):
+            return idx[:, cols.start // 16 : cols.stop // 16]
+
+        def halves(n):
+            return [slice(0, n // 2), slice(n // 2, n)]
 
         def look_up(move, t):
-            half = C // 2
-            for h in range(2):
-                move(met[t][:, h * half : (h + 1) * half], pv[t][:].indirect(meet[:, h * half // 16 : (h + 1) * half // 16]))
+            for cols in halves(C):
+                move(met[t][:, cols], pv[t][:].indirect(listed(meet, cols)))
 
         def keep_larger(t):
             nc.vector.tensor_tensor(pg[t][:], pw[t][:], met[t][:], MAX)
 
-        def read_out(move, t):
-            move(hid[:, t, :], pg[t][:].indirect(read[:]))
+        def read_out(move, t, cols):
+            move(hid[:, t, cols], pg[t][:].indirect(listed(read, cols)))
 
-        nc.scalar.copy(b_sb[0][:], b_banks[0][:])
-        put(on_scalar, pv, b_sb, put_b, 0)
-        nc.vector.tensor_copy(a_sb[0][:], a_banks[0][:])
-        put(on_scalar, pv, b_sb, put_b, 1)
-        put(on_vector, pw, a_sb, put_a, 0)
-        look_up(on_scalar, 0)
-        put(on_vector, pw, a_sb, put_a, 1)
-        nc.scalar.copy(b_sb[1][:], b_banks[1][:])
-        keep_larger(0)
-        look_up(on_scalar, 1)
-        nc.vector.tensor_copy(a_sb[1][:], a_banks[1][:])
-        put(on_scalar, pv, b_sb, put_b, 2)
-        put(on_vector, pw, a_sb, put_a, 2)
-        keep_larger(1)
-        read_out(on_scalar, 0)
-        put(on_scalar, pv, b_sb, put_b, 3)
-        put(on_vector, pw, a_sb, put_a, 3)
-        look_up(on_scalar, 2)
-        look_up(on_vector, 3)
-        read_out(on_scalar, 1)
-        keep_larger(2)
-        keep_larger(3)
-        read_out(on_scalar, 2)
-        read_out(on_vector, 3)
+        whole = slice(0, O)
+        empty(nc.scalar.copy, b_copies[0])
+        empty(nc.scalar.copy, b_copies[1])
+        empty(on_vector, b_copies[2])
+        empty(on_vector, a_copies[0])
+        nc.vector.tensor_copy(vg_w[:], vs_w[:].indirect(entry[:]))
+        empty(on_vector, a_copies[1])
+        nc.vector.tensor_copy(vg_s[:], vs_s[:].indirect(entry[:]))
+        for t in range(PACK):
+            put(on_scalar, pv, b, put_b, t)
+            put(on_vector, pw, a, put_a, t)
+        for t in range(PACK):
+            look_up(on_scalar, t)
+            keep_larger(t)
+        for t in range(PACK):
+            read_out(on_vector if t == PACK - 1 else on_scalar, t, whole)
 
         grouped = sb.tile([P, O, PACK], BF16, name="grouped", align_bytes=64)
-        nc.vector.tensor_copy(grouped[:], hid[:].rearrange("p t o -> p o t"))
         h_w = sb.tile([P, O], U32, name="h_w", align_bytes=64)
         h_s = sb.tile([P, O], U8, name="h_s", align_bytes=64)
-        nc.vector.quantize_mx(h_w[:].bitcast(E5M2), h_s[:], grouped[:].rearrange("p o t -> p (o t)"))
+        for cols in halves(O):
+            nc.vector.tensor_copy(grouped[:, cols, :], hid[:, :, cols].rearrange("p t o -> p o t"))
+        for cols in halves(O):
+            nc.vector.quantize_mx(h_w[:, cols].bitcast(E5M2), h_s[:, cols], grouped[:, cols, :].rearrange("p o t -> p (o t)"))
 
+        y_banks = [ps.tile([P, O], F32, name=f"y_bank{h}") for h in range(2)]
+        for cols in halves(O):
+            for bank, rows in zip(y_banks, halves(N)):
+                nc.tensor.matmul_mx(
+                    bank[:, cols],
+                    lhsT=vg_w[:, rows].bitcast(E2M1),
+                    lhsT_scale=vg_s[:, rows],
+                    rhs=h_w[:, cols].bitcast(E5M2),
+                    rhs_scale=h_s[:, cols],
+                    start=True,
+                    stop=True,
+                )
         for h, (copy_out, queue) in enumerate(((nc.vector.tensor_copy, nc.sync), (nc.scalar.copy, nc.scalar))):
-            cols = slice(h * P, (h + 1) * P)
-            bank = ps.tile([P, O], F32, name=f"y_bank{h}")
-            nc.tensor.matmul_mx(
-                bank[:],
-                lhsT=vg_w[:, cols].bitcast(E2M1),
-                lhsT_scale=vg_s[:, cols],
-                rhs=h_w[:].bitcast(E5M2),
-                rhs_scale=h_s[:],
-                start=True,
-                stop=True,
-            )
             y = sb.tile([P, O], F32, name=f"y{h}")
-            copy_out(y[:], bank[:])
-            queue.dma_start(out[cols, :], y[:])
+            copy_out(y[:], y_banks[h][:])
+            queue.dma_start(out[halves(N)[h], :], y[:])

@@ -16,6 +16,7 @@ MAX = mybir.AluOpType.max
 
 P = 128
 PACK = 4
+SPARE = 16
 K, T, J, R, C, D, O, N, S = 512, 2048, 256, 512, 512, 512, 256, 256, 1024
 
 FLOPS = 2 * K * R * 2 * J + 2 * R * N * O
@@ -43,11 +44,11 @@ def tile_list_boardsmeet_tied_store_plain_kernel(
         xt_s = sb.tile([P, T], U8, name="xt_s", align_bytes=64)
         w_w = sb.tile([P, R], U32, name="w_w", align_bytes=64)
         w_s = sb.tile([P, R], U8, name="w_s", align_bytes=64)
-        vs_w = sb.tile([P, S], U16, name="vs_w", align_bytes=64)
+        vs_w = sb.tile([P, S], U16, name="vs_w", tag="after_store", align_bytes=64)
         vs_s = sb.tile([P, S], U8, name="vs_s", align_bytes=64)
 
+        nc.vector.memset(w_s[:].bitcast(I32), 0)
         nc.vector.memset(xt_s[:].bitcast(I32), 0)
-        nc.gpsimd.memset(w_s[:].bitcast(I32), 0)
         idx_b = load_list(offs2, "idx_b")
         load_scales(w_s, w_scales, (0, 1))
         nc.sync.dma_start(xt_w[:].bitcast(I32), xt_words[0].bitcast(I32))
@@ -64,16 +65,15 @@ def tile_list_boardsmeet_tied_store_plain_kernel(
         meet = load_list(offs5, "meet")
         read = load_list(offs6, "read")
 
-        pv = [sb.tile([P, D], F32, name=f"pv{t}") for t in range(PACK)]
+        pv = [sb.tile([P, D + SPARE], F32, name=f"pv{t}") for t in range(PACK)]
         pw = [sb.tile([P, C], F32, name=f"pw{t}") for t in range(PACK)]
-        for t in range(PACK):
-            nc.vector.memset(pv[t][:], 0.0)
-            nc.gpsimd.memset(pw[t][:], 0.0)
+        for board in pv + pw:
+            nc.vector.memset(board[:], 0.0)
 
         wp_w = sb.tile([P, PACK, P], U32, name="wp_w", align_bytes=64)
         wp_s = sb.tile([P, PACK, P], U8, name="wp_s", align_bytes=64)
         nc.scalar.copy(wp_w[:].rearrange("p t m -> p m t"), w_w[:].rearrange("p (m t) -> p m t", t=PACK))
-        nc.vector.tensor_copy(wp_s[:].rearrange("p t m -> p m t"), w_s[:].rearrange("p (m t) -> p m t", t=PACK))
+        nc.vector.tensor_copy(wp_s[:], w_s[:].rearrange("p (m t) -> p t m", t=PACK))
 
         def pick(words, scales, idx, name):
             gw = sb.tile([P, J], U16, name=name + "_w", align_bytes=64)
@@ -82,15 +82,14 @@ def tile_list_boardsmeet_tied_store_plain_kernel(
             nc.vector.tensor_copy(gs[:], scales[:].indirect(idx[:]))
             return gw, gs
 
-        def first_stage(gw, gs, name, groups):
+        def first_stage(gw, gs, name, held):
             sums, copies, parts = [], [], []
-            for g, size in enumerate(groups):
-                bank = ps.tile([P, size, J], F32, name=f"{name}_bank{g}")
-                held = sb.tile([P, size, J], F32, name=f"{name}_sb{g}")
-                copies.append((held, bank))
-                for i in range(size):
+            for g, dst in enumerate(held):
+                bank = ps.tile(list(dst.shape), F32, name=f"{name}_bank{g}")
+                copies.append((dst, bank[:]))
+                for i in range(dst.shape[1]):
                     sums.append(bank[:, i, :])
-                    parts.append(held[:, i, :])
+                    parts.append(dst[:, i, :])
             for t in range(PACK):
                 nc.tensor.matmul_mx(
                     sums[t],
@@ -103,8 +102,10 @@ def tile_list_boardsmeet_tied_store_plain_kernel(
                 )
             return copies, parts
 
-        b_copies, b = first_stage(*pick(xt_w, xt_s, idx_b, "xb"), "b", (1, 1, 2))
-        a_copies, a = first_stage(*pick(xt_w, xt_s, idx_a, "xa"), "a", (2, 2))
+        early = sb.tile([P, 2, J], F32, name="early")
+        middle = sb.tile([P, 6, J], F32, name="middle", tag="after_store", align_bytes=64)
+        b_copies, b = first_stage(*pick(xt_w, xt_s, idx_b, "xb"), "b", (early[:, 0:1, :], early[:, 1:2, :], middle[:, 0:2, :]))
+        a_copies, a = first_stage(*pick(xt_w, xt_s, idx_a, "xa"), "a", (middle[:, 2:4, :], middle[:, 4:6, :]))
         vg_w = sb.tile([P, N], U16, name="vg_w", align_bytes=64)
         vg_s = sb.tile([P, N], U8, name="vg_s", align_bytes=64)
 
@@ -118,7 +119,7 @@ def tile_list_boardsmeet_tied_store_plain_kernel(
         on_vector = nc.vector.tensor_copy
 
         def empty(move, pair):
-            move(pair[0][:], pair[1][:])
+            move(*pair)
 
         def put(move, board, values, idx, t):
             move(board[t][:].indirect(idx[:]), values[t])
@@ -130,8 +131,7 @@ def tile_list_boardsmeet_tied_store_plain_kernel(
             return [slice(0, n // 2), slice(n // 2, n)]
 
         def look_up(move, t):
-            for cols in halves(C):
-                move(met[t][:, cols], pv[t][:].indirect(listed(meet, cols)))
+            move(met[t][:], pv[t][:].indirect(meet[:]))
 
         def keep_larger(t):
             nc.vector.tensor_tensor(pg[t][:], pw[t][:], met[t][:], MAX)
@@ -139,36 +139,36 @@ def tile_list_boardsmeet_tied_store_plain_kernel(
         def read_out(move, t, cols):
             move(hid[:, t, cols], pg[t][:].indirect(listed(read, cols)))
 
-        whole = slice(0, O)
         empty(nc.scalar.copy, b_copies[0])
         empty(nc.scalar.copy, b_copies[1])
+        nc.vector.tensor_copy(vg_w[:], vs_w[:].indirect(entry[:]))
         empty(on_vector, b_copies[2])
         empty(on_vector, a_copies[0])
-        nc.vector.tensor_copy(vg_w[:], vs_w[:].indirect(entry[:]))
-        empty(on_vector, a_copies[1])
         nc.vector.tensor_copy(vg_s[:], vs_s[:].indirect(entry[:]))
+        empty(on_vector, a_copies[1])
         for t in range(PACK):
             put(on_scalar, pv, b, put_b, t)
             put(on_vector, pw, a, put_a, t)
         for t in range(PACK):
             look_up(on_scalar, t)
             keep_larger(t)
-        for t in range(PACK):
-            read_out(on_vector if t == PACK - 1 else on_scalar, t, whole)
+        for cols in halves(O):
+            for t in range(PACK):
+                read_out(on_vector if t == PACK - 1 else on_scalar, t, cols)
 
         grouped = sb.tile([P, O, PACK], BF16, name="grouped", align_bytes=64)
         h_w = sb.tile([P, O], U32, name="h_w", align_bytes=64)
         h_s = sb.tile([P, O], U8, name="h_s", align_bytes=64)
-        for cols in halves(O):
-            nc.vector.tensor_copy(grouped[:, cols, :], hid[:, :, cols].rearrange("p t o -> p o t"))
-        for cols in halves(O):
-            nc.vector.quantize_mx(h_w[:, cols].bitcast(E5M2), h_s[:, cols], grouped[:, cols, :].rearrange("p o t -> p (o t)"))
 
-        y_banks = [ps.tile([P, O], F32, name=f"y_bank{h}") for h in range(2)]
-        for cols in halves(O):
-            for bank, rows in zip(y_banks, halves(N)):
+        def second_stage(sums, cols):
+            nc.vector.tensor_copy(
+                grouped[:, cols, :].rearrange("p (c i) t -> p c t i", i=4),
+                hid[:, :, cols].rearrange("p t (c i) -> p c t i", i=4),
+            )
+            nc.vector.quantize_mx(h_w[:, cols].bitcast(E5M2), h_s[:, cols], grouped[:, cols, :].rearrange("p o t -> p (o t)"))
+            for acc, rows in zip(sums, halves(N)):
                 nc.tensor.matmul_mx(
-                    bank[:, cols],
+                    acc,
                     lhsT=vg_w[:, rows].bitcast(E2M1),
                     lhsT_scale=vg_s[:, rows],
                     rhs=h_w[:, cols].bitcast(E5M2),
@@ -176,7 +176,17 @@ def tile_list_boardsmeet_tied_store_plain_kernel(
                     start=True,
                     stop=True,
                 )
-        for h, (copy_out, queue) in enumerate(((nc.vector.tensor_copy, nc.sync), (nc.scalar.copy, nc.scalar))):
-            y = sb.tile([P, O], F32, name=f"y{h}")
-            copy_out(y[:], y_banks[h][:])
-            queue.dma_start(out[halves(N)[h], :], y[:])
+
+        first, last = halves(O)
+        y_first_bank = ps.tile([P, 2, O // 2], F32, name="y_first_bank")
+        second_stage([y_first_bank[:, h, :] for h in range(2)], first)
+        y_first = sb.tile([P, 2, O // 2], F32, name="y_first")
+        nc.scalar.copy(y_first[:], y_first_bank[:])
+        nc.sync.dma_start(out[:, first].rearrange("(h p) o -> p h o", p=P), y_first[:])
+
+        y_last_banks = [ps.tile([P, O // 2], F32, name=f"y_last_bank{h}") for h in range(2)]
+        second_stage([bank[:] for bank in y_last_banks], last)
+        for h, (copy_out, queue) in enumerate(((nc.scalar.copy, nc.scalar), (nc.vector.tensor_copy, nc.sync))):
+            y_last = sb.tile([P, O // 2], F32, name=f"y_last{h}")
+            copy_out(y_last[:], y_last_banks[h][:])
+            queue.dma_start(out[halves(N)[h], last], y_last[:])

@@ -70,9 +70,13 @@ def tile_list_boardsmeet_tied_store_plain_kernel(
         for board in pv + pw:
             nc.vector.memset(board[:], 0.0)
 
-        wp_w = sb.tile([P, PACK, P], U32, name="wp_w", align_bytes=64)
+        wp_first = sb.tile([P, P], U32, name="wp_first", align_bytes=64)
+        wp_rest = sb.tile([P, PACK - 1, P], U32, name="wp_rest", align_bytes=64)
+        wp_w = [wp_first[:]] + [wp_rest[:, t, :] for t in range(PACK - 1)]
         wp_s = sb.tile([P, PACK, P], U8, name="wp_s", align_bytes=64)
-        nc.scalar.copy(wp_w[:].rearrange("p t m -> p m t"), w_w[:].rearrange("p (m t) -> p m t", t=PACK))
+        w_by_m = w_w[:].rearrange("p (m t) -> p m t", t=PACK)
+        nc.scalar.copy(wp_first[:], w_by_m[:, :, 0])
+        nc.scalar.copy(wp_rest[:].rearrange("p t m -> p m t"), w_by_m[:, :, 1:])
         nc.vector.tensor_copy(wp_s[:], w_s[:].rearrange("p (m t) -> p t m", t=PACK))
 
         def pick(words, scales, idx, name):
@@ -82,7 +86,7 @@ def tile_list_boardsmeet_tied_store_plain_kernel(
             nc.vector.tensor_copy(gs[:], scales[:].indirect(idx[:]))
             return gw, gs
 
-        def first_stage(gw, gs, name, held):
+        def first_stage(gw, gs, name, order, held):
             sums, copies, parts = [], [], []
             for g, dst in enumerate(held):
                 bank = ps.tile(list(dst.shape), F32, name=f"{name}_bank{g}")
@@ -90,10 +94,10 @@ def tile_list_boardsmeet_tied_store_plain_kernel(
                 for i in range(dst.shape[1]):
                     sums.append(bank[:, i, :])
                     parts.append(dst[:, i, :])
-            for t in range(PACK):
+            for t in order:
                 nc.tensor.matmul_mx(
                     sums[t],
-                    lhsT=wp_w[:, t, :].bitcast(E4M3),
+                    lhsT=wp_w[t].bitcast(E4M3),
                     lhsT_scale=wp_s[:, t, :],
                     rhs=gw[:].bitcast(E2M1),
                     rhs_scale=gs[:],
@@ -104,8 +108,8 @@ def tile_list_boardsmeet_tied_store_plain_kernel(
 
         early = sb.tile([P, 2, J], F32, name="early")
         middle = sb.tile([P, 6, J], F32, name="middle", tag="after_store", align_bytes=64)
-        b_copies, b = first_stage(*pick(xt_w, xt_s, idx_b, "xb"), "b", (early[:, 0:1, :], early[:, 1:2, :], middle[:, 0:2, :]))
-        a_copies, a = first_stage(*pick(xt_w, xt_s, idx_a, "xa"), "a", (middle[:, 2:4, :], middle[:, 4:6, :]))
+        b_copies, b = first_stage(*pick(xt_w, xt_s, idx_b, "xb"), "b", (0, 1, 2, 3), (early[:, 0:1, :], early[:, 1:2, :], middle[:, 0:2, :]))
+        a_copies, a = first_stage(*pick(xt_w, xt_s, idx_a, "xa"), "a", (1, 0, 2, 3), (middle[:, 2:4, :], middle[:, 4:6, :]))
         vg_w = sb.tile([P, N], U16, name="vg_w", align_bytes=64)
         vg_s = sb.tile([P, N], U8, name="vg_s", align_bytes=64)
 

from contextlib import ExitStack

import concourse.mybir as mybir

F32 = mybir.dt.float32
BF16 = mybir.dt.bfloat16
I32 = mybir.dt.int32
U32 = mybir.dt.uint32
U16 = mybir.dt.uint16
U8 = mybir.dt.uint8
E4M3 = mybir.dt.float8_e4m3fn_x4
E5M2 = mybir.dt.float8_e5m2_x4
E2M1 = mybir.dt.float4_e2m1fn_x4
COPY = mybir.ActivationFunctionType.Copy
MAX = mybir.AluOpType.max

P = 128
PACK = 4
SPARE = 16
K, T, J, R, C, D, O, N, S = 512, 2048, 256, 512, 512, 512, 256, 256, 1024

FLOPS = 2 * K * R * 2 * J + 2 * R * N * O


def tile_list_boardsmeet_tied_store_plain_kernel(
    tc, xt_words, xt_scales, w_words, w_scales, vs_words, vs_scales, offs, offs2, offs3, offs4, offs5, offs6, offs7, out
):
    nc = tc.nc
    with ExitStack() as ctx:
        lists = ctx.enter_context(tc.tile_pool(name="lists", bufs=1))
        sb = ctx.enter_context(tc.tile_pool(name="sb", bufs=1))
        ps = ctx.enter_context(tc.psum_pool(name="ps", bufs=1))

        def load_list(src, name):
            tile = lists.tile([P, src.shape[1]], U16, name=name)
            nc.sync.dma_start(tile[:], src)
            return tile

        def load_scales(tile, src, quadrants):
            for q in quadrants:
                nc.sync.dma_start(tile[32 * q : 32 * q + 4, :].bitcast(I32), src[0, 4 * q : 4 * q + 4, :].bitcast(I32))

        xt_w = sb.tile([P, T], U16, name="xt_w", align_bytes=64)
        xt_s = sb.tile([P, T], U8, name="xt_s", align_bytes=64)
        w_w = sb.tile([P, R], U32, name="w_w", align_bytes=64)
        w_s = sb.tile([P, R], U8, name="w_s", align_bytes=64)
        vs_w = sb.tile([P, S], U16, name="vs_w", tag="after_store", align_bytes=64)
        vs_s = sb.tile([P, S], U8, name="vs_s", align_bytes=64)

        nc.vector.memset(w_s[:].bitcast(I32), 0)
        nc.vector.memset(xt_s[:].bitcast(I32), 0)
        idx_b = load_list(offs2, "idx_b")
        load_scales(w_s, w_scales, (0, 1))
        nc.sync.dma_start(xt_w[:].bitcast(I32), xt_words[0].bitcast(I32))
        load_scales(xt_s, xt_scales, range(4))
        nc.sync.dma_start(w_w[:].bitcast(I32), w_words[0].rearrange("p n t -> p (n t)").bitcast(I32))
        load_scales(w_s, w_scales, (2, 3))
        idx_a = load_list(offs, "idx_a")
        put_b = load_list(offs4, "put_b")
        entry = load_list(offs7, "entry")
        nc.vector.memset(vs_s[:].bitcast(I32), 0)
        nc.sync.dma_start(vs_w[:].bitcast(I32), vs_words[0].bitcast(I32))
        load_scales(vs_s, vs_scales, range(4))
        put_a = load_list(offs3, "put_a")
        meet = load_list(offs5, "meet")
        read = load_list(offs6, "read")

        pv = [sb.tile([P, D + SPARE], F32, name=f"pv{t}") for t in range(PACK)]
        pw = [sb.tile([P, C], F32, name=f"pw{t}") for t in range(PACK)]
        for board in pv + pw:
            nc.vector.memset(board[:], 0.0)

        wp_first = sb.tile([P, P], U32, name="wp_first", align_bytes=64)
        wp_rest = sb.tile([P, PACK - 1, P], U32, name="wp_rest", align_bytes=64)
        wp_w = [wp_first[:]] + [wp_rest[:, t, :] for t in range(PACK - 1)]
        wp_s = sb.tile([P, PACK, P], U8, name="wp_s", align_bytes=64)
        w_by_m = w_w[:].rearrange("p (m t) -> p m t", t=PACK)
        nc.scalar.copy(wp_first[:], w_by_m[:, :, 0])
        nc.scalar.copy(wp_rest[:].rearrange("p t m -> p m t"), w_by_m[:, :, 1:])
        nc.vector.tensor_copy(wp_s[:], w_s[:].rearrange("p (m t) -> p t m", t=PACK))

        def pick(words, scales, idx, name):
            gw = sb.tile([P, J], U16, name=name + "_w", align_bytes=64)
            gs = sb.tile([P, J], U8, name=name + "_s", align_bytes=64)
            nc.vector.tensor_copy(gw[:], words[:].indirect(idx[:]))
            nc.vector.tensor_copy(gs[:], scales[:].indirect(idx[:]))
            return gw, gs

        def first_stage(gw, gs, name, order, held):
            sums, copies, parts = [], [], []
            for g, dst in enumerate(held):
                bank = ps.tile(list(dst.shape), F32, name=f"{name}_bank{g}")
                copies.append((dst, bank[:]))
                for i in range(dst.shape[1]):
                    sums.append(bank[:, i, :])
                    parts.append(dst[:, i, :])
            for t in order:
                nc.tensor.matmul_mx(
                    sums[t],
                    lhsT=wp_w[t].bitcast(E4M3),
                    lhsT_scale=wp_s[:, t, :],
                    rhs=gw[:].bitcast(E2M1),
                    rhs_scale=gs[:],
                    start=True,
                    stop=True,
                )
            return copies, parts

        early = sb.tile([P, 2, J], F32, name="early")
        middle = sb.tile([P, 6, J], F32, name="middle", tag="after_store", align_bytes=64)
        b_copies, b = first_stage(*pick(xt_w, xt_s, idx_b, "xb"), "b", (0, 1, 2, 3), (early[:, 0:1, :], early[:, 1:2, :], middle[:, 0:2, :]))
        a_copies, a = first_stage(*pick(xt_w, xt_s, idx_a, "xa"), "a", (1, 0, 2, 3), (middle[:, 2:4, :], middle[:, 4:6, :]))
        vg_w = sb.tile([P, N], U16, name="vg_w", align_bytes=64)
        vg_s = sb.tile([P, N], U8, name="vg_s", align_bytes=64)

        met = [sb.tile([P, C], F32, name=f"met{t}") for t in range(PACK)]
        pg = [sb.tile([P, C], F32, name=f"pg{t}") for t in range(PACK)]
        hid = sb.tile([P, PACK, O], F32, name="hid")

        def on_scalar(dst, src):
            nc.scalar.activation(dst, src, COPY)

        on_vector = nc.vector.tensor_copy

        def empty(move, pair):
            move(*pair)

        def put(move, board, values, idx, t):
            move(board[t][:].indirect(idx[:]), values[t])

        def listed(idx, cols):
            return idx[:, cols.start // 16 : cols.stop // 16]

        def halves(n):
            return [slice(0, n // 2), slice(n // 2, n)]

        def look_up(move, t):
            move(met[t][:], pv[t][:].indirect(meet[:]))

        def keep_larger(t):
            nc.vector.tensor_tensor(pg[t][:], pw[t][:], met[t][:], MAX)

        def read_out(move, t, cols):
            move(hid[:, t, cols], pg[t][:].indirect(listed(read, cols)))

        empty(nc.scalar.copy, b_copies[0])
        empty(nc.scalar.copy, b_copies[1])
        nc.vector.tensor_copy(vg_w[:], vs_w[:].indirect(entry[:]))
        empty(on_vector, b_copies[2])
        empty(on_vector, a_copies[0])
        nc.vector.tensor_copy(vg_s[:], vs_s[:].indirect(entry[:]))
        empty(on_vector, a_copies[1])
        for t in range(PACK):
            put(on_scalar, pv, b, put_b, t)
            put(on_vector, pw, a, put_a, t)
        for t in range(PACK):
            look_up(on_scalar, t)
            keep_larger(t)
        for cols in halves(O):
            for t in range(PACK):
                read_out(on_vector if t == PACK - 1 else on_scalar, t, cols)

        grouped = sb.tile([P, O, PACK], BF16, name="grouped", align_bytes=64)
        h_w = sb.tile([P, O], U32, name="h_w", align_bytes=64)
        h_s = sb.tile([P, O], U8, name="h_s", align_bytes=64)

        def second_stage(sums, cols):
            nc.vector.tensor_copy(
                grouped[:, cols, :].rearrange("p (c i) t -> p c t i", i=4),
                hid[:, :, cols].rearrange("p t (c i) -> p c t i", i=4),
            )
            nc.vector.quantize_mx(h_w[:, cols].bitcast(E5M2), h_s[:, cols], grouped[:, cols, :].rearrange("p o t -> p (o t)"))
            for acc, rows in zip(sums, halves(N)):
                nc.tensor.matmul_mx(
                    acc,
                    lhsT=vg_w[:, rows].bitcast(E2M1),
                    lhsT_scale=vg_s[:, rows],
                    rhs=h_w[:, cols].bitcast(E5M2),
                    rhs_scale=h_s[:, cols],
                    start=True,
                    stop=True,
                )

        first, last = halves(O)
        y_first_bank = ps.tile([P, 2, O // 2], F32, name="y_first_bank")
        second_stage([y_first_bank[:, h, :] for h in range(2)], first)
        y_first = sb.tile([P, 2, O // 2], F32, name="y_first")
        nc.scalar.copy(y_first[:], y_first_bank[:])
        nc.sync.dma_start(out[:, first].rearrange("(h p) o -> p h o", p=P), y_first[:])

        y_last_banks = [ps.tile([P, O // 2], F32, name=f"y_last_bank{h}") for h in range(2)]
        second_stage([bank[:] for bank in y_last_banks], last)
        for h, (copy_out, queue) in enumerate(((nc.scalar.copy, nc.scalar), (nc.vector.tensor_copy, nc.sync))):
            y_last = sb.tile([P, O // 2], F32, name=f"y_last{h}")
            copy_out(y_last[:], y_last_banks[h][:])
            queue.dma_start(out[halves(N)[h], last], y_last[:])
